import numpy as np, ml_dtypes
CORES = [30,158,46,174,86,214]
N = 6
WB, KB, QP = 3, 1, 512
def setup_inputs(rng):
    return {"q": rng.standard_normal((N, 128, QP), dtype=np.float32).astype(ml_dtypes.bfloat16), "k": rng.standard_normal((N, 128, KB * 128), dtype=np.float32).astype(ml_dtypes.bfloat16), "v": rng.standard_normal((N, 128, KB * 128), dtype=np.float32).astype(ml_dtypes.bfloat16)}
def setup_inputs_big(rng):
    d = setup_inputs(rng)
    for k in ("q", "k", "v"): d[k] = (d[k].astype(np.float32) * 1024.0).astype(d[k].dtype)
    return d
def setup_inputs_small(rng):
    d = setup_inputs(rng)
    for k in ("q", "k", "v"): d[k] = (d[k].astype(np.float32) * (1 / 1024.0)).astype(d[k].dtype)
    return d
def setup_inputs_apart(rng):
    d = setup_inputs(rng)
    f = (10.0 ** rng.permutation(np.linspace(-1.5, 1.5, N))).astype(np.float32).reshape(N, 1, 1)
    for k in ("q", "k", "v"): d[k] = (d[k].astype(np.float32) * f).astype(d[k].dtype)
    return d
def reference(q, k, v):
    Q, K, V = q.astype(np.float64), k.astype(np.float64), v.astype(np.float64)
    y = np.zeros((N, 128, QP))
    for r in range(N):
        for j in range(max(0, r - WB), r + 1):
            for b in range(KB):
                S = np.maximum(K[j][:, 128 * b:128 * b + 128].T @ Q[r], 0.0)
                y[r] += V[j][:, 128 * b:128 * b + 128].T @ S
    return {"y": y.astype(ml_dtypes.bfloat16 if q.dtype != np.float64 else np.float64)}

@@ -1,0 +1,109 @@
+from concourse.mybir import AluOpType
+
+WB = 3
+KP, QP = 128, 512
+KVW = 2 * KP
+NCH = 2
+W = QP // NCH
+NPS = 8 - NCH
+SEND_ORDER = (1, 2, 3)
+RECV_ORDER = (1, 2, 3)
+
+SCRATCH = {
+    "kv": ("sbuf", [128, KVW], "bfloat16"),
+    "kvin": ("sbuf", [128, WB * KVW], "bfloat16"),
+    "qs": ("sbuf", [128, QP], "bfloat16"),
+    "zero": ("sbuf", [128, W], "float32"),
+    "sb": ("sbuf", [128, (WB + 1) * QP], "bfloat16"),
+    "yb": ("sbuf", [128, QP], "bfloat16"),
+}
+for _c in range(NCH):
+    SCRATCH["po%d" % _c] = ("psum", [128, 512], "float32")
+for _c in range(NPS):
+    SCRATCH["ps%d" % _c] = ("psum", [128, 512], "float32")
+
+SEMAPHORES = ["kvld", "qld", "zs", "sent", "st"]
+SEMAPHORES += ["arr%d" % s for s in range(WB)]
+SEMAPHORES += ["m1_%d_%d" % (i, c) for i in range(WB + 1) for c in range(NCH)]
+SEMAPHORES += ["rl_%d_%d" % (i, c) for i in range(WB + 1) for c in range(NCH)]
+SEMAPHORES += ["m2_%d" % c for c in range(NCH)]
+SEMAPHORES += ["cp_%d" % c for c in range(NCH)]
+
+
+def _count(mask):
+    return bin(mask).count("1")
+
+
+def rank_program(g, core, T, topo):
+    r = T.rank_of(core)
+    if r is None:
+        return
+    n = len(T.cores)
+    sem = T.sem
+    te, ve, sy, sc = g.tensor, g.vector, g.sync, g.scalar
+    dests = [d for d in SEND_ORDER if r + d < n]
+    srcs = [d for d in RECV_ORDER if r - d >= 0]
+
+    sy.dma_start(T.kv[:, 0:KP], T.k[:]).then_inc(sem.kvld, 16)
+    sc.dma_start(T.kv[:, KP:KVW], T.v[:]).then_inc(sem.kvld, 16)
+    h = QP // 2
+    sy.dma_start(T.qs[:, 0:h], T.q[:, 0:h]).then_inc(sem.qld, 16)
+    sc.dma_start(T.qs[:, h:QP], T.q[:, h:QP]).then_inc(sem.qld, 16)
+
+    slot = r % WB
+    sent = 0
+    if dests:
+        g.wait_ge(sem.kvld, 32)
+    for d in dests:
+        dst = T.cores[r + d]
+        if not topo.may_write(core, dst):
+            raise ValueError("core %d may not write to core %d" % (core, dst))
+        rid, pid = topo.addr(dst, core)
+        mask = topo.mask(core, dst)
+        g.remote_dma(out_ap=T.kvin[:, slot * KVW:(slot + 1) * KVW], in_ap=T.kv[:], remote_sem=sem["arr%d" % slot],
+                     local_sem=sem.sent, pid=pid, routing_id=rid, dma_engine_mask=mask)
+        sent += _count(mask)
+
+    blocks = [(None, 0, T.kv[:, 0:KP], T.kv[:, KP:KVW])]
+    for d in srcs:
+        src = T.cores[r - d]
+        s = (r - d) % WB
+        blocks.append((sem["arr%d" % s], _count(topo.mask(src, core)),
+                       T.kvin[:, s * KVW:s * KVW + KP], T.kvin[:, s * KVW + KP:(s + 1) * KVW]))
+    last = len(blocks) - 1
+
+    te.wait_ge(sem.kvld, 32)
+    te.wait_ge(sem.qld, 32)
+    for i, (asem, acnt, k_ap, v_ap) in enumerate(blocks):
+        if asem is not None:
+            te.wait_ge(asem, acnt)
+        for c in range(NCH):
+            ps = T["ps%d" % ((i * NCH + c) % NPS)]
+            te.matmul(ps[:, 0:W], k_ap, T.qs[:, c * W:(c + 1) * W], True, True).then_inc(sem["m1_%d_%d" % (i, c)], 1)
+        for c in range(NCH):
+            o = (i * NCH + c) * W
+            te.wait_ge(sem["rl_%d_%d" % (i, c)], 1)
+            mm = te.matmul(T["po%d" % c][:, 0:W], v_ap, T.sb[:, o:o + W], i == 0, i == last)
+            if i == last:
+                mm.then_inc(sem["m2_%d" % c], 1)
+
+    ve.memset(T.zero[:], 0.0).then_inc(sem.zs, 1)
+    ve.wait_ge(sem.zs, 1)
+    for i in range(len(blocks)):
+        for c in range(NCH):
+            ps = T["ps%d" % ((i * NCH + c) % NPS)]
+            o = (i * NCH + c) * W
+            ve.wait_ge(sem["m1_%d_%d" % (i, c)], 1)
+            ve.tensor_tensor(T.sb[:, o:o + W], ps[:, 0:W], T.zero[:], AluOpType.max).then_inc(sem["rl_%d_%d" % (i, c)], 1)
+    for c in range(NCH):
+        ve.wait_ge(sem["m2_%d" % c], 1)
+        ve.tensor_copy(T.yb[:, c * W:(c + 1) * W], T["po%d" % c][:, 0:W]).then_inc(sem["cp_%d" % c], 1)
+
+    for c in range(NCH):
+        qd = sy if c % 2 == 0 else sc
+        qd.wait_ge(sem["cp_%d" % c], 1)
+        qd.dma_start(T.y[:, c * W:(c + 1) * W], T.yb[:, c * W:(c + 1) * W]).then_inc(sem.st, 16)
+
+    if sent:
+        g.wait_ge(sem.sent, sent)
+    g.wait_ge(sem.st, 16 * NCH)

@@ -6,8 +6,8 @@ KVW = 2 * KP
 NCH = 2
 W = QP // NCH
 NPS = 8 - NCH
-SEND_ORDER = (1, 2, 3)
-RECV_ORDER = (1, 2, 3)
+ORDER = (1, 2, 3)
+SPLIT = 3
 
 SCRATCH = {
     "kv": ("sbuf", [128, KVW], "bfloat16"),
@@ -22,7 +22,7 @@ for _c in range(NCH):
 for _c in range(NPS):
     SCRATCH["ps%d" % _c] = ("psum", [128, 512], "float32")
 
-SEMAPHORES = ["kvld", "qld", "zs", "sent", "st"]
+SEMAPHORES = ["kvld", "qld", "zs", "sent", "st", "ark", "arv"]
 SEMAPHORES += ["arr%d" % s for s in range(WB)]
 SEMAPHORES += ["m1_%d_%d" % (i, c) for i in range(WB + 1) for c in range(NCH)]
 SEMAPHORES += ["rl_%d_%d" % (i, c) for i in range(WB + 1) for c in range(NCH)]
@@ -41,8 +41,6 @@ def rank_program(g, core, T, topo):
     n = len(T.cores)
     sem = T.sem
     te, ve, sy, sc = g.tensor, g.vector, g.sync, g.scalar
-    dests = [d for d in SEND_ORDER if r + d < n]
-    srcs = [d for d in RECV_ORDER if r - d >= 0]
 
     sy.dma_start(T.kv[:, 0:KP], T.k[:]).then_inc(sem.kvld, 16)
     sc.dma_start(T.kv[:, KP:KVW], T.v[:]).then_inc(sem.kvld, 16)
@@ -50,42 +48,69 @@ def rank_program(g, core, T, topo):
     sy.dma_start(T.qs[:, 0:h], T.q[:, 0:h]).then_inc(sem.qld, 16)
     sc.dma_start(T.qs[:, h:QP], T.q[:, h:QP]).then_inc(sem.qld, 16)
 
-    slot = r % WB
+    base = (r % WB) * KVW
     sent = 0
-    if dests:
-        g.wait_ge(sem.kvld, 32)
-    for d in dests:
+    for d in ORDER:
+        if r + d >= n:
+            continue
         dst = T.cores[r + d]
         if not topo.may_write(core, dst):
             raise ValueError("core %d may not write to core %d" % (core, dst))
         rid, pid = topo.addr(dst, core)
         mask = topo.mask(core, dst)
-        g.remote_dma(out_ap=T.kvin[:, slot * KVW:(slot + 1) * KVW], in_ap=T.kv[:], remote_sem=sem["arr%d" % slot],
-                     local_sem=sem.sent, pid=pid, routing_id=rid, dma_engine_mask=mask)
-        sent += _count(mask)
+        if d == SPLIT:
+            pieces = (("ark", 0, KP), ("arv", KP, KVW))
+        else:
+            pieces = (("arr%d" % (r % WB), 0, KVW),)
+        if not sent:
+            g.wait_ge(sem.kvld, 32)
+        for name, lo, hi in pieces:
+            g.remote_dma(out_ap=T.kvin[:, base + lo:base + hi], in_ap=T.kv[:, lo:hi], remote_sem=sem[name],
+                         local_sem=sem.sent, pid=pid, routing_id=rid, dma_engine_mask=mask)
+            sent += _count(mask)
 
-    blocks = [(None, 0, T.kv[:, 0:KP], T.kv[:, KP:KVW])]
-    for d in srcs:
-        src = T.cores[r - d]
+    blocks = [(None, None, 0, T.kv[:, 0:KP], T.kv[:, KP:KVW])]
+    for d in ORDER:
+        if r - d < 0:
+            continue
         s = (r - d) % WB
-        blocks.append((sem["arr%d" % s], _count(topo.mask(src, core)),
-                       T.kvin[:, s * KVW:s * KVW + KP], T.kvin[:, s * KVW + KP:(s + 1) * KVW]))
+        cnt = _count(topo.mask(T.cores[r - d], core))
+        k_ap, v_ap = T.kvin[:, s * KVW:s * KVW + KP], T.kvin[:, s * KVW + KP:(s + 1) * KVW]
+        if d == SPLIT:
+            blocks.append((sem.ark, sem.arv, cnt, k_ap, v_ap))
+        else:
+            blocks.append((sem["arr%d" % s], None, cnt, k_ap, v_ap))
     last = len(blocks) - 1
 
-    te.wait_ge(sem.kvld, 32)
-    te.wait_ge(sem.qld, 32)
-    for i, (asem, acnt, k_ap, v_ap) in enumerate(blocks):
-        if asem is not None:
-            te.wait_ge(asem, acnt)
+    def scores(i):
+        ksem, _, cnt, k_ap, _ = blocks[i]
+        if ksem is not None:
+            te.wait_ge(ksem, cnt)
         for c in range(NCH):
             ps = T["ps%d" % ((i * NCH + c) % NPS)]
             te.matmul(ps[:, 0:W], k_ap, T.qs[:, c * W:(c + 1) * W], True, True).then_inc(sem["m1_%d_%d" % (i, c)], 1)
+
+    def values(i):
+        _, vsem, cnt, _, v_ap = blocks[i]
+        if vsem is not None:
+            te.wait_ge(vsem, cnt)
         for c in range(NCH):
             o = (i * NCH + c) * W
             te.wait_ge(sem["rl_%d_%d" % (i, c)], 1)
             mm = te.matmul(T["po%d" % c][:, 0:W], v_ap, T.sb[:, o:o + W], i == 0, i == last)
             if i == last:
                 mm.then_inc(sem["m2_%d" % c], 1)
+
+    te.wait_ge(sem.kvld, 32)
+    te.wait_ge(sem.qld, 32)
+    scores(0)
+    values(0)
+    for i in range(1, last + 1):
+        scores(i)
+        if i > 1:
+            values(i - 1)
+    if last > 0:
+        values(last)
 
     ve.memset(T.zero[:], 0.0).then_inc(sem.zs, 1)
     ve.wait_ge(sem.zs, 1)

from concourse.mybir import AluOpType

WB = 3
KP, QP = 128, 512
KVW = 2 * KP
NCH = 2
W = QP // NCH
NPS = 8 - NCH
ORDER = (1, 2, 3)
SPLIT = 3

SCRATCH = {
    "kv": ("sbuf", [128, KVW], "bfloat16"),
    "kvin": ("sbuf", [128, WB * KVW], "bfloat16"),
    "qs": ("sbuf", [128, QP], "bfloat16"),
    "zero": ("sbuf", [128, W], "float32"),
    "sb": ("sbuf", [128, (WB + 1) * QP], "bfloat16"),
    "yb": ("sbuf", [128, QP], "bfloat16"),
}
for _c in range(NCH):
    SCRATCH["po%d" % _c] = ("psum", [128, 512], "float32")
for _c in range(NPS):
    SCRATCH["ps%d" % _c] = ("psum", [128, 512], "float32")

SEMAPHORES = ["kvld", "qld", "zs", "sent", "st", "ark", "arv"]
SEMAPHORES += ["arr%d" % s for s in range(WB)]
SEMAPHORES += ["m1_%d_%d" % (i, c) for i in range(WB + 1) for c in range(NCH)]
SEMAPHORES += ["rl_%d_%d" % (i, c) for i in range(WB + 1) for c in range(NCH)]
SEMAPHORES += ["m2_%d" % c for c in range(NCH)]
SEMAPHORES += ["cp_%d" % c for c in range(NCH)]


def _count(mask):
    return bin(mask).count("1")


def rank_program(g, core, T, topo):
    r = T.rank_of(core)
    if r is None:
        return
    n = len(T.cores)
    sem = T.sem
    te, ve, sy, sc = g.tensor, g.vector, g.sync, g.scalar

    sy.dma_start(T.kv[:, 0:KP], T.k[:]).then_inc(sem.kvld, 16)
    sc.dma_start(T.kv[:, KP:KVW], T.v[:]).then_inc(sem.kvld, 16)
    h = QP // 2
    sy.dma_start(T.qs[:, 0:h], T.q[:, 0:h]).then_inc(sem.qld, 16)
    sc.dma_start(T.qs[:, h:QP], T.q[:, h:QP]).then_inc(sem.qld, 16)

    base = (r % WB) * KVW
    sent = 0
    for d in ORDER:
        if r + d >= n:
            continue
        dst = T.cores[r + d]
        if not topo.may_write(core, dst):
            raise ValueError("core %d may not write to core %d" % (core, dst))
        rid, pid = topo.addr(dst, core)
        mask = topo.mask(core, dst)
        if d == SPLIT:
            pieces = (("ark", 0, KP), ("arv", KP, KVW))
        else:
            pieces = (("arr%d" % (r % WB), 0, KVW),)
        if not sent:
            g.wait_ge(sem.kvld, 32)
        for name, lo, hi in pieces:
            g.remote_dma(out_ap=T.kvin[:, base + lo:base + hi], in_ap=T.kv[:, lo:hi], remote_sem=sem[name],
                         local_sem=sem.sent, pid=pid, routing_id=rid, dma_engine_mask=mask)
            sent += _count(mask)

    blocks = [(None, None, 0, T.kv[:, 0:KP], T.kv[:, KP:KVW])]
    for d in ORDER:
        if r - d < 0:
            continue
        s = (r - d) % WB
        cnt = _count(topo.mask(T.cores[r - d], core))
        k_ap, v_ap = T.kvin[:, s * KVW:s * KVW + KP], T.kvin[:, s * KVW + KP:(s + 1) * KVW]
        if d == SPLIT:
            blocks.append((sem.ark, sem.arv, cnt, k_ap, v_ap))
        else:
            blocks.append((sem["arr%d" % s], None, cnt, k_ap, v_ap))
    last = len(blocks) - 1

    def scores(i):
        ksem, _, cnt, k_ap, _ = blocks[i]
        if ksem is not None:
            te.wait_ge(ksem, cnt)
        for c in range(NCH):
            ps = T["ps%d" % ((i * NCH + c) % NPS)]
            te.matmul(ps[:, 0:W], k_ap, T.qs[:, c * W:(c + 1) * W], True, True).then_inc(sem["m1_%d_%d" % (i, c)], 1)

    def values(i):
        _, vsem, cnt, _, v_ap = blocks[i]
        if vsem is not None:
            te.wait_ge(vsem, cnt)
        for c in range(NCH):
            o = (i * NCH + c) * W
            te.wait_ge(sem["rl_%d_%d" % (i, c)], 1)
            mm = te.matmul(T["po%d" % c][:, 0:W], v_ap, T.sb[:, o:o + W], i == 0, i == last)
            if i == last:
                mm.then_inc(sem["m2_%d" % c], 1)

    te.wait_ge(sem.kvld, 32)
    te.wait_ge(sem.qld, 32)
    scores(0)
    values(0)
    for i in range(1, last + 1):
        scores(i)
        if i > 1:
            values(i - 1)
    if last > 0:
        values(last)

    ve.memset(T.zero[:], 0.0).then_inc(sem.zs, 1)
    ve.wait_ge(sem.zs, 1)
    for i in range(len(blocks)):
        for c in range(NCH):
            ps = T["ps%d" % ((i * NCH + c) % NPS)]
            o = (i * NCH + c) * W
            ve.wait_ge(sem["m1_%d_%d" % (i, c)], 1)
            ve.tensor_tensor(T.sb[:, o:o + W], ps[:, 0:W], T.zero[:], AluOpType.max).then_inc(sem["rl_%d_%d" % (i, c)], 1)
    for c in range(NCH):
        ve.wait_ge(sem["m2_%d" % c], 1)
        ve.tensor_copy(T.yb[:, c * W:(c + 1) * W], T["po%d" % c][:, 0:W]).then_inc(sem["cp_%d" % c], 1)

    for c in range(NCH):
        qd = sy if c % 2 == 0 else sc
        qd.wait_ge(sem["cp_%d" % c], 1)
        qd.dma_start(T.y[:, c * W:(c + 1) * W], T.yb[:, c * W:(c + 1) * W]).then_inc(sem.st, 16)

    if sent:
        g.wait_ge(sem.sent, sent)
    g.wait_ge(sem.st, 16 * NCH)
